import numpy as np
import ml_dtypes


def mxq(x, axis, fmt="e4m3"):
    dtype, down = {"e4m3": (ml_dtypes.float8_e4m3fn, 7), "e5m2": (ml_dtypes.float8_e5m2, 14)}[fmt]
    v = np.moveaxis(np.asarray(x, np.float32).astype(ml_dtypes.bfloat16).astype(np.float64), axis, -1)
    blocks = v.reshape(v.shape[:-1] + (-1, 32))
    amax = np.abs(blocks).max(-1, keepdims=True)
    byte = np.maximum(np.where(amax > 0, np.frexp(amax)[1] - 1 + 127, 0) - down, 1)
    scale = np.exp2(byte - 127.0)
    codes = (blocks / scale).astype(np.float32).astype(dtype).astype(np.float64)
    return np.moveaxis((codes * scale).reshape(v.shape), -1, axis)


WIDE = False


def mx_kscale(k):
    if not WIDE:
        return np.ones(k)
    levels = np.array([10, -10, 5, -5, 0])
    if k % 512:
        return np.exp2(np.random.permutation(np.resize(levels, k // 32))).repeat(32)
    a = np.empty((k // 512, 16))
    for p in range(k // 512):
        a[p, :8] = np.random.permutation(np.resize(levels, 8))
        for g in range(8):
            far = levels[np.abs(levels - a[p, g]) >= 10]
            a[p, g + 8] = far[np.random.randint(len(far))]
    return np.exp2(a.ravel()).repeat(32)


def f64(x):
    return np.asarray(x).astype(np.float64)


def striped8(idx):
    return np.asarray(idx).reshape(8, -1, 16).transpose(0, 2, 1).reshape(128, -1).astype(np.uint16)


def unstriped8(offs):
    return offs.reshape(8, 16, -1).transpose(0, 2, 1).reshape(8, -1).astype(np.int64)


def pick8(x, idx, run):
    r = np.arange(len(x))
    return x[r[:, None], idx[r % (8 * run) // run]]


E2M1 = np.array([0.0, 0.5, 1.0, 1.5, 2.0, 3.0, 4.0, 6.0, -0.0, -0.5, -1.0, -1.5, -2.0, -3.0, -4.0, -6.0])


def pack_weight(w, fmt):
    k, n = w.shape
    w = f64(np.asarray(w, np.float32).astype(ml_dtypes.bfloat16)).reshape(k // 32, 32, n)
    amax = np.abs(w).max(1)
    if fmt == "e4m3":
        byte = np.frexp(amax)[1] - 1 + 127 - 7
    else:
        mant, ex = np.frexp(amax / 6.0)
        byte = np.where(mant > 0.5, ex, ex - 1) + 127
    byte = np.clip(np.where(amax > 0, byte, 1), 1, 254)
    scaled = (w * np.exp2(127.0 - byte)[:, None, :]).reshape(k, n).astype(np.float32)
    by_word = np.ascontiguousarray(scaled.reshape(k // 512, 128, 4, n).transpose(0, 1, 3, 2))
    if fmt == "e4m3":
        words = by_word.astype(ml_dtypes.float8_e4m3fn).view(np.uint8)
    else:
        c = by_word.astype(ml_dtypes.float4_e2m1fn).view(np.uint8) & 0xF
        words = (c[..., 0::2] | (c[..., 1::2] << 4)).reshape(k // 512, 128, 2 * n)
    return np.ascontiguousarray(words), np.ascontiguousarray(byte.astype(np.uint8).reshape(k // 512, 16, n))


def unpack_weight(words, scales, fmt):
    g, _, n = scales.shape
    words = np.ascontiguousarray(words).reshape(g, 128, n, -1)
    if fmt == "e4m3":
        vals = words.view(ml_dtypes.float8_e4m3fn).astype(np.float64)
    else:
        nib = np.empty((g, 128, n, 4), np.uint8)
        nib[..., 0::2] = words & 0xF
        nib[..., 1::2] = words >> 4
        vals = E2M1[nib]
    vals = vals * np.repeat(np.exp2(scales.astype(np.float64) - 127.0), 8, axis=1)[..., None]
    return vals.transpose(0, 1, 3, 2).reshape(g * 512, n)


D, T, I, Q = 512, 1024, 512, 128


def setup_inputs():
    n = np.random.standard_normal
    idx = np.stack([np.random.permutation(T)[:I] for _ in range(8)])
    idx2 = np.stack([np.random.permutation(T)[:I] for _ in range(8)])
    fd = mx_kscale(D)
    keysp = pack_weight(n((D, T)) / fd[:, None], "e4m3")
    return {
        "query": (n((D, Q)) * 0.9 / np.sqrt(D) * fd[:, None]).astype(np.float32),
        "query2": (n((D, Q)) * 0.9 / np.sqrt(D) * fd[:, None]).astype(np.float32),
        "keys_words": keysp[0],
        "keys_scales": keysp[1],
        "lam": (np.random.uniform(0.5, 1.3, (Q, 1))).astype(np.float32),
        "smear": (np.random.uniform(0.3, 0.8, (Q, 1))).astype(np.float32),
        "base": (0.3 * n((Q, I))).astype(np.float32),
        "gain2": (np.random.uniform(0.5, 2.0, (Q, 1))).astype(np.float32),
        "offs": striped8(idx),
        "offs2": striped8(idx2),
    }


def reference(query, query2, keys_words, keys_scales, lam, smear, base, gain2, offs, offs2):
    idx = unstriped8(offs)
    idx2 = unstriped8(offs2)
    keysu = unpack_weight(keys_words, keys_scales, "e4m3")
    queryq = mxq(f64(query), 0, "e4m3")
    a = queryq.T @ keysu
    query2q = mxq(f64(query2), 0, "e4m3")
    b = query2q.T @ keysu
    s = (np.maximum(pick8(a, idx, 16), pick8(b, idx2, 16)) - np.maximum(pick8(a, idx2, 16), pick8(b, idx, 16))) * f64(lam)
    p = np.exp(s - np.max(s, axis=1, keepdims=True))
    r = p / np.sum(p, axis=1, keepdims=True)
    r1 = np.pad(r, ((0, 0), (1, 0)))[:, :I]
    r2 = np.pad(r, ((0, 0), (2, 0)))[:, :I]
    w = r + r1 * f64(smear) + r2 * np.square(f64(smear))
    y = np.tanh(w * f64(gain2) * 128.0) + f64(base)
    return y

@@ -1,0 +1,171 @@
+from contextlib import ExitStack
+
+import concourse.mybir as mybir
+
+D, T, I, Q = 512, 1024, 512, 128
+FLOPS = 2 * 2 * D * T * Q
+
+F32 = mybir.dt.float32
+BF16 = mybir.dt.bfloat16
+I32 = mybir.dt.int32
+U32 = mybir.dt.uint32
+U16 = mybir.dt.uint16
+U8 = mybir.dt.uint8
+FP8X4 = mybir.dt.float8_e4m3fn_x4
+ALU = mybir.AluOpType
+ACT = mybir.ActivationFunctionType
+
+P = 128
+PACK = 4
+N_MM = 256
+HALF = 256
+PAD = 8
+
+
+def tile_attend_exchanged_smeared_gated_heads_kernel(
+    tc, query, query2, keys_words, keys_scales, lam, smear, base, gain2, offs, offs2, out
+):
+    nc = tc.nc
+    with ExitStack() as ctx:
+        pool = ctx.enter_context(tc.tile_pool(name="pool", bufs=1))
+        psum = ctx.enter_context(tc.psum_pool(name="psum", bufs=1))
+
+        key_scales = pool.tile([P, T], U8, name="key_scales", align_bytes=64)
+        nc.vector.memset(key_scales[:].bitcast(I32), 0)
+        p_pad = pool.tile([P, PAD + I], F32, name="p_pad")
+        nc.vector.memset(p_pad[:, 0:PAD], 0.0)
+
+        raw = [pool.tile([P, PACK, Q], F32, name="raw%d" % s) for s in range(2)]
+        words = [pool.tile([P, T // 2], I32, name="words%d" % h, align_bytes=64) for h in range(2)]
+        words_hbm = keys_words[0].rearrange("p n t -> p (n t)").bitcast(I32)
+        scales_hbm = keys_scales[0].bitcast(I32)
+
+        nc.sync.dma_start(out=raw[0][:], in_=query.rearrange("(p j) q -> p j q", j=PACK))
+        for quad in range(4):
+            nc.sync.dma_start(
+                out=key_scales[32 * quad : 32 * quad + 4, :].bitcast(I32), in_=scales_hbm[4 * quad : 4 * quad + 4, :]
+            )
+        nc.sync.dma_start(out=words[0][:], in_=words_hbm[:, 0 : T // 2])
+        nc.sync.dma_start(out=raw[1][:], in_=query2.rearrange("(p j) q -> p j q", j=PACK))
+        nc.sync.dma_start(out=words[1][:], in_=words_hbm[:, T // 2 : T])
+        first = pool.tile([P, I // 16], U16, name="first")
+        second = pool.tile([P, I // 16], U16, name="second")
+        nc.sync.dma_start(first[:], offs)
+        nc.sync.dma_start(second[:], offs2)
+        lam_sb = pool.tile([P, 1], F32, name="lam_sb")
+        smear_sb = pool.tile([P, 1], F32, name="smear_sb")
+        gain_sb = pool.tile([P, 1], F32, name="gain_sb")
+        base_sb = pool.tile([P, I], F32, name="base_sb")
+        nc.sync.dma_start(out=lam_sb[:], in_=lam)
+        nc.sync.dma_start(out=smear_sb[:], in_=smear)
+        nc.sync.dma_start(out=gain_sb[:], in_=gain2)
+        nc.sync.dma_start(out=base_sb[:], in_=base)
+
+        scores = [pool.tile([P, T], F32, name="scores%d" % s) for s in range(2)]
+        for s in range(2):
+            grouped = pool.tile([P, Q, PACK], BF16, name="grouped%d" % s, align_bytes=64)
+            nc.vector.tensor_copy(
+                out=grouped[:].rearrange("p (c i) j -> p c j i", i=4),
+                in_=raw[s][:].rearrange("p j (c i) -> p c j i", i=4),
+            )
+            codes = pool.tile([P, Q], U32, name="codes%d" % s, align_bytes=64)
+            q_scales = pool.tile([P, Q], U8, name="q_scales%d" % s, align_bytes=64)
+            nc.vector.quantize_mx(
+                out=codes[:].bitcast(FP8X4), scales=q_scales[:], in_=grouped[:].rearrange("p q j -> p (q j)")
+            )
+            for c in range(T // N_MM):
+                h, c0 = divmod(c * N_MM, T // 2)
+                bank = psum.tile([P, N_MM], F32, name="bank%d_%d" % (s, c))
+                nc.tensor.matmul_mx(
+                    out=bank[:],
+                    lhsT=codes[:].bitcast(FP8X4),
+                    lhsT_scale=q_scales[:],
+                    rhs=words[h][:, c0 : c0 + N_MM].bitcast(FP8X4),
+                    rhs_scale=key_scales[:, c * N_MM : (c + 1) * N_MM],
+                    start=True,
+                    stop=True,
+                )
+                nc.scalar.copy(out=scores[s][:, c * N_MM : (c + 1) * N_MM], in_=bank[:])
+
+        a, b = scores
+        neg = pool.tile([P, I], F32, name="neg")
+        low = [pool.tile([P, 1], F32, name="low%d" % h) for h in range(2)]
+        cols16 = HALF // 16
+
+        def gather(on_vector, name, window, lst, h):
+            got = pool.tile([P, HALF], F32, name=name)
+            src = window[:].indirect(lst[:, h * cols16 : (h + 1) * cols16])
+            if on_vector:
+                nc.vector.tensor_copy(out=got[:], in_=src)
+            else:
+                nc.scalar.activation(out=got[:], in_=src, func=ACT.Copy)
+            return got
+
+        for h in range(2):
+            a1 = gather(h == 0, "a1_%d" % h, a, first, h)
+            a2 = gather(h == 0, "a2_%d" % h, a, second, h)
+            b2 = gather(True, "b2_%d" % h, b, second, h)
+            b1 = gather(False, "b1_%d" % h, b, first, h)
+            m1 = pool.tile([P, HALF], F32, name="m1_%d" % h)
+            m2 = pool.tile([P, HALF], F32, name="m2_%d" % h)
+            diff = pool.tile([P, HALF], F32, name="diff_%d" % h)
+            nc.vector.tensor_tensor(out=m1[:], in0=a1[:], in1=b2[:], op=ALU.max)
+            nc.vector.tensor_tensor(out=m2[:], in0=a2[:], in1=b1[:], op=ALU.max)
+            nc.vector.tensor_tensor(out=diff[:], in0=m2[:], in1=m1[:], op=ALU.subtract)
+            nc.vector.tensor_scalar(
+                out=neg[:, h * HALF : (h + 1) * HALF],
+                in0=diff[:],
+                scalar1=lam_sb[:],
+                scalar2=None if h == 0 else low[0][:],
+                op0=ALU.mult,
+                op1=ALU.min,
+                accum_out=low[h][:],
+            )
+
+        sums = [pool.tile([P, 1], F32, name="sum%d" % h) for h in range(2)]
+        weights = []
+        for h in range(2):
+            c0 = h * HALF
+            nc.scalar.activation(
+                out=p_pad[:, PAD + c0 : PAD + c0 + HALF],
+                in_=neg[:, c0 : c0 + HALF],
+                func=ACT.Exp,
+                bias=low[1][:],
+                scale=-1.0,
+                accum_out=sums[h][:],
+            )
+            back = pool.tile([P, HALF], F32, name="back%d" % h)
+            nc.vector.scalar_tensor_tensor(
+                out=back[:],
+                in0=p_pad[:, PAD - 2 + c0 : PAD - 2 + c0 + HALF],
+                scalar=smear_sb[:],
+                in1=p_pad[:, PAD - 1 + c0 : PAD - 1 + c0 + HALF],
+                op0=ALU.mult,
+                op1=ALU.add,
+            )
+            w = pool.tile([P, HALF], F32, name="w%d" % h)
+            nc.vector.scalar_tensor_tensor(
+                out=w[:],
+                in0=back[:],
+                scalar=smear_sb[:],
+                in1=p_pad[:, PAD + c0 : PAD + c0 + HALF],
+                op0=ALU.mult,
+                op1=ALU.add,
+            )
+            weights.append(w)
+            if h == 0:
+                total = pool.tile([P, 1], F32, name="total")
+        nc.vector.tensor_tensor(out=total[:], in0=sums[0][:], in1=sums[1][:], op=ALU.add)
+        inv = pool.tile([P, 1], F32, name="inv")
+        nc.vector.reciprocal(out=inv[:], in_=total[:])
+        factor = pool.tile([P, 1], F32, name="factor")
+        nc.vector.tensor_scalar(
+            out=factor[:], in0=inv[:], scalar1=gain_sb[:], scalar2=128.0, op0=ALU.mult, op1=ALU.mult
+        )
+        for h in range(2):
+            c0 = h * HALF
+            th = pool.tile([P, HALF], F32, name="th%d" % h)
+            nc.scalar.activation(out=th[:], in_=weights[h][:], func=ACT.Tanh, scale=factor[:])
+            res = pool.tile([P, HALF], F32, name="res%d" % h)
+            nc.vector.tensor_tensor(out=res[:], in0=th[:], in1=base_sb[:, c0 : c0 + HALF], op=ALU.add)
+            nc.sync.dma_start(out=out[:, c0 : c0 + HALF], in_=res[:])

@@ -17,9 +17,11 @@ ACT = mybir.ActivationFunctionType
 
 P = 128
 PACK = 4
-N_MM = 256
-HALF = 256
+QUARTER = T // 4
+HALF = I // 2
+REACH = 2
 PAD = 8
+LIST_ROWS = 16
 
 
 def tile_attend_exchanged_smeared_gated_heads_kernel(
@@ -30,142 +32,175 @@ def tile_attend_exchanged_smeared_gated_heads_kernel(
         pool = ctx.enter_context(tc.tile_pool(name="pool", bufs=1))
         psum = ctx.enter_context(tc.psum_pool(name="psum", bufs=1))
 
-        key_scales = pool.tile([P, T], U8, name="key_scales", align_bytes=64)
+        def wide(name):
+            return pool.tile([P, HALF], F32, name=name)
+
+        def column(name):
+            return pool.tile([P, 1], F32, name=name)
+
+        key_scales = pool.tile([P, QUARTER], U8, name="key_scales", align_bytes=64)
         nc.vector.memset(key_scales[:].bitcast(I32), 0)
-        p_pad = pool.tile([P, PAD + I], F32, name="p_pad")
-        nc.vector.memset(p_pad[:, 0:PAD], 0.0)
 
         raw = [pool.tile([P, PACK, Q], F32, name="raw%d" % s) for s in range(2)]
         words = [pool.tile([P, T // 2], I32, name="words%d" % h, align_bytes=64) for h in range(2)]
         words_hbm = keys_words[0].rearrange("p n t -> p (n t)").bitcast(I32)
         scales_hbm = keys_scales[0].bitcast(I32)
-
         nc.sync.dma_start(out=raw[0][:], in_=query.rearrange("(p j) q -> p j q", j=PACK))
-        for quad in range(4):
-            nc.sync.dma_start(
-                out=key_scales[32 * quad : 32 * quad + 4, :].bitcast(I32), in_=scales_hbm[4 * quad : 4 * quad + 4, :]
-            )
         nc.sync.dma_start(out=words[0][:], in_=words_hbm[:, 0 : T // 2])
+        for r in range(4):
+            nc.sync.dma_start(
+                out=key_scales[32 * r : 32 * r + 16, :].bitcast(I32),
+                in_=scales_hbm[4 * r : 4 * r + 4, :].rearrange("j (c n) -> c j n", c=4),
+            )
         nc.sync.dma_start(out=raw[1][:], in_=query2.rearrange("(p j) q -> p j q", j=PACK))
         nc.sync.dma_start(out=words[1][:], in_=words_hbm[:, T // 2 : T])
-        first = pool.tile([P, I // 16], U16, name="first")
-        second = pool.tile([P, I // 16], U16, name="second")
+        first = pool.tile([P, I // LIST_ROWS], U16, name="first")
+        second = pool.tile([P, I // LIST_ROWS], U16, name="second")
         nc.sync.dma_start(first[:], offs)
         nc.sync.dma_start(second[:], offs2)
-        lam_sb = pool.tile([P, 1], F32, name="lam_sb")
-        smear_sb = pool.tile([P, 1], F32, name="smear_sb")
-        gain_sb = pool.tile([P, 1], F32, name="gain_sb")
+        lam_sb, smear_sb, gain_sb = column("lam_sb"), column("smear_sb"), column("gain_sb")
         base_sb = pool.tile([P, I], F32, name="base_sb")
         nc.sync.dma_start(out=lam_sb[:], in_=lam)
         nc.sync.dma_start(out=smear_sb[:], in_=smear)
         nc.sync.dma_start(out=gain_sb[:], in_=gain2)
         nc.sync.dma_start(out=base_sb[:], in_=base)
 
-        scores = [pool.tile([P, T], F32, name="scores%d" % s) for s in range(2)]
-        for s in range(2):
+        shares = [pool.tile([P, PAD + HALF + h], F32, name="shares%d" % h) for h in range(2)]
+        nc.vector.memset(shares[0][:, PAD - REACH : PAD], 0.0)
+
+        def quantise(s):
             grouped = pool.tile([P, Q, PACK], BF16, name="grouped%d" % s, align_bytes=64)
-            nc.vector.tensor_copy(
-                out=grouped[:].rearrange("p (c i) j -> p c j i", i=4),
-                in_=raw[s][:].rearrange("p j (c i) -> p c j i", i=4),
-            )
             codes = pool.tile([P, Q], U32, name="codes%d" % s, align_bytes=64)
             q_scales = pool.tile([P, Q], U8, name="q_scales%d" % s, align_bytes=64)
-            nc.vector.quantize_mx(
-                out=codes[:].bitcast(FP8X4), scales=q_scales[:], in_=grouped[:].rearrange("p q j -> p (q j)")
-            )
-            for c in range(T // N_MM):
-                h, c0 = divmod(c * N_MM, T // 2)
-                bank = psum.tile([P, N_MM], F32, name="bank%d_%d" % (s, c))
+            runs = [slice(0, Q // 2), slice(Q // 2, Q)]
+            for rows in runs:
+                nc.vector.tensor_copy(
+                    out=grouped[:, rows, :].rearrange("p (c i) j -> p c j i", i=4),
+                    in_=raw[s][:, :, rows].rearrange("p j (c i) -> p c j i", i=4),
+                )
+            for rows in runs:
+                nc.vector.quantize_mx(
+                    out=codes[:, rows].bitcast(FP8X4),
+                    scales=q_scales[:, rows],
+                    in_=grouped[:, rows, :].rearrange("p q j -> p (q j)"),
+                )
+            return codes, q_scales
+
+        def score(s, operand, copiers):
+            codes, q_scales = operand
+            table = pool.tile([P, T], F32, name="scores%d" % s)
+            for c, copier in enumerate(copiers):
+                h, c0 = divmod(c * QUARTER, T // 2)
+                bank = psum.tile([P, QUARTER], F32, name="bank%d_%d" % (s, c))
                 nc.tensor.matmul_mx(
                     out=bank[:],
                     lhsT=codes[:].bitcast(FP8X4),
                     lhsT_scale=q_scales[:],
-                    rhs=words[h][:, c0 : c0 + N_MM].bitcast(FP8X4),
-                    rhs_scale=key_scales[:, c * N_MM : (c + 1) * N_MM],
+                    rhs=words[h][:, c0 : c0 + QUARTER].bitcast(FP8X4),
+                    rhs_scale=key_scales[4 * c : P, :],
                     start=True,
                     stop=True,
                 )
-                nc.scalar.copy(out=scores[s][:, c * N_MM : (c + 1) * N_MM], in_=bank[:])
+                copier(out=table[:, c * QUARTER : (c + 1) * QUARTER], in_=bank[:])
+            return table
 
-        a, b = scores
-        neg = pool.tile([P, I], F32, name="neg")
-        low = [pool.tile([P, 1], F32, name="low%d" % h) for h in range(2)]
-        cols16 = HALF // 16
+        def listed(table, lists, i0, i1):
+            return table[:].indirect(lists[:, i0 // LIST_ROWS : i1 // LIST_ROWS])
 
-        def gather(on_vector, name, window, lst, h):
-            got = pool.tile([P, HALF], F32, name=name)
-            src = window[:].indirect(lst[:, h * cols16 : (h + 1) * cols16])
-            if on_vector:
-                nc.vector.tensor_copy(out=got[:], in_=src)
-            else:
-                nc.scalar.activation(out=got[:], in_=src, func=ACT.Copy)
+        def gather_on_vector(name, table, lists):
+            got = pool.tile([P, I], F32, name=name)
+            nc.vector.tensor_copy(out=got[:], in_=listed(table, lists, 0, I))
             return got
 
-        for h in range(2):
-            a1 = gather(h == 0, "a1_%d" % h, a, first, h)
-            a2 = gather(h == 0, "a2_%d" % h, a, second, h)
-            b2 = gather(True, "b2_%d" % h, b, second, h)
-            b1 = gather(False, "b1_%d" % h, b, first, h)
-            m1 = pool.tile([P, HALF], F32, name="m1_%d" % h)
-            m2 = pool.tile([P, HALF], F32, name="m2_%d" % h)
-            diff = pool.tile([P, HALF], F32, name="diff_%d" % h)
-            nc.vector.tensor_tensor(out=m1[:], in0=a1[:], in1=b2[:], op=ALU.max)
-            nc.vector.tensor_tensor(out=m2[:], in0=a2[:], in1=b1[:], op=ALU.max)
-            nc.vector.tensor_tensor(out=diff[:], in0=m2[:], in1=m1[:], op=ALU.subtract)
+        def gather_on_scalar(name, table, lists, i0, i1):
+            got = pool.tile([P, i1 - i0], F32, name=name)
+            nc.scalar.activation(out=got[:], in_=listed(table, lists, i0, i1), func=ACT.Copy)
+            return got
+
+        on_scalar, on_vector = nc.scalar.copy, nc.vector.tensor_copy
+        operands = [quantise(s) for s in range(2)]
+        a = score(0, operands[0], [on_scalar, on_scalar, on_scalar, on_vector])
+        a_first = gather_on_vector("a_first", a, first)
+        b = score(1, operands[1], [on_scalar] * 4)
+        a_second = gather_on_scalar("a_second", a, second, 0, I)
+        b_second = gather_on_vector("b_second", b, second)
+        b_first = [gather_on_scalar("b_first%d" % h, b, first, h * HALF, (h + 1) * HALF) for h in range(2)]
+
+        neg = pool.tile([P, I + 1], F32, name="neg")
+        low = [neg[:, I : I + 1], column("row_low")[:]]
+        sums = [column("sum%d" % h) for h in range(2)]
+        halves = [slice(h * HALF, (h + 1) * HALF) for h in range(2)]
+
+        def combine(name, x, y, op):
+            z = wide(name)
+            nc.vector.tensor_tensor(out=z[:], in0=x, in1=y, op=op)
+            return z
+
+        def straight(h):
+            return combine("straight%d" % h, a_first[:, halves[h]], b_second[:, halves[h]], ALU.max)
+
+        def crossed(h):
+            return combine("crossed%d" % h, a_second[:, halves[h]], b_first[h][:], ALU.max)
+
+        def scale_and_min(h, diff):
             nc.vector.tensor_scalar(
-                out=neg[:, h * HALF : (h + 1) * HALF],
+                out=neg[:, halves[h]],
                 in0=diff[:],
                 scalar1=lam_sb[:],
-                scalar2=None if h == 0 else low[0][:],
+                scalar2=low[0] if h else None,
                 op0=ALU.mult,
                 op1=ALU.min,
-                accum_out=low[h][:],
+                accum_out=low[h],
             )
 
-        sums = [pool.tile([P, 1], F32, name="sum%d" % h) for h in range(2)]
-        weights = []
-        for h in range(2):
-            c0 = h * HALF
-            nc.scalar.activation(
-                out=p_pad[:, PAD + c0 : PAD + c0 + HALF],
-                in_=neg[:, c0 : c0 + HALF],
-                func=ACT.Exp,
-                bias=low[1][:],
-                scale=-1.0,
-                accum_out=sums[h][:],
-            )
-            back = pool.tile([P, HALF], F32, name="back%d" % h)
+        def exp_of(dst, src, h, accum=None):
+            nc.scalar.activation(out=dst, in_=src, func=ACT.Exp, bias=low[h], scale=-1.0, accum_out=accum)
+
+        def smear_step(name, older, newer):
+            z = wide(name)
             nc.vector.scalar_tensor_tensor(
-                out=back[:],
-                in0=p_pad[:, PAD - 2 + c0 : PAD - 2 + c0 + HALF],
-                scalar=smear_sb[:],
-                in1=p_pad[:, PAD - 1 + c0 : PAD - 1 + c0 + HALF],
-                op0=ALU.mult,
-                op1=ALU.add,
+                out=z[:], in0=older, scalar=smear_sb[:], in1=newer, op0=ALU.mult, op1=ALU.add
             )
-            w = pool.tile([P, HALF], F32, name="w%d" % h)
-            nc.vector.scalar_tensor_tensor(
-                out=w[:],
-                in0=back[:],
-                scalar=smear_sb[:],
-                in1=p_pad[:, PAD + c0 : PAD + c0 + HALF],
-                op0=ALU.mult,
-                op1=ALU.add,
-            )
-            weights.append(w)
-            if h == 0:
-                total = pool.tile([P, 1], F32, name="total")
-        nc.vector.tensor_tensor(out=total[:], in0=sums[0][:], in1=sums[1][:], op=ALU.add)
-        inv = pool.tile([P, 1], F32, name="inv")
+            return z
+
+        def shifted(h, shift):
+            return shares[h][:, PAD - shift : PAD - shift + HALF]
+
+        straight_0 = straight(0)
+        straight_1 = straight(1)
+        crossed_0 = crossed(0)
+        diff_0 = combine("diff0", crossed_0[:], straight_0[:], ALU.subtract)
+        crossed_1 = crossed(1)
+        scale_and_min(0, diff_0)
+        own = HALF - REACH
+        exp_of(shares[0][:, PAD : PAD + own], neg[:, 0:own], 0, sums[0][:])
+        exp_of(shares[0][:, PAD + own : PAD + HALF], neg[:, own:HALF], 0)
+        diff_1 = combine("diff1", crossed_1[:], straight_1[:], ALU.subtract)
+        scale_and_min(1, diff_1)
+
+        back_0 = smear_step("back0", shifted(0, 2), shifted(0, 1))
+        rest = column("rest")
+        nc.vector.tensor_scalar(out=rest[:], in0=sums[0][:], scalar1=-1.0, scalar2=None, op0=ALU.add)
+        exp_of(shares[1][:, PAD - REACH : PAD + HALF + 1], neg[:, own : I + 1], 1, sums[1][:])
+        shrink = shares[1][:, PAD + HALF : PAD + HALF + 1]
+        w_0 = smear_step("w0", back_0[:], shifted(0, 0))
+        gain128 = column("gain128")
+        nc.vector.tensor_scalar(out=gain128[:], in0=gain_sb[:], scalar1=128.0, scalar2=None, op0=ALU.mult)
+        total = column("total")
+        nc.scalar.activation(out=total[:], in_=rest[:], func=ACT.Identity, scale=shrink, bias=sums[1][:])
+        back_1 = smear_step("back1", shifted(1, 2), shifted(1, 1))
+        inv = column("inv")
         nc.vector.reciprocal(out=inv[:], in_=total[:])
-        factor = pool.tile([P, 1], F32, name="factor")
+        scaled_0 = wide("scaled0")
         nc.vector.tensor_scalar(
-            out=factor[:], in0=inv[:], scalar1=gain_sb[:], scalar2=128.0, op0=ALU.mult, op1=ALU.mult
+            out=scaled_0[:], in0=w_0[:], scalar1=gain128[:], scalar2=shrink, op0=ALU.mult, op1=ALU.mult
         )
-        for h in range(2):
-            c0 = h * HALF
-            th = pool.tile([P, HALF], F32, name="th%d" % h)
-            nc.scalar.activation(out=th[:], in_=weights[h][:], func=ACT.Tanh, scale=factor[:])
-            res = pool.tile([P, HALF], F32, name="res%d" % h)
-            nc.vector.tensor_tensor(out=res[:], in0=th[:], in1=base_sb[:, c0 : c0 + HALF], op=ALU.add)
-            nc.sync.dma_start(out=out[:, c0 : c0 + HALF], in_=res[:])
+        w_1 = smear_step("w1", back_1[:], shifted(1, 0))
+        factor = column("factor")
+        nc.scalar.activation(out=factor[:], in_=inv[:], func=ACT.Copy, scale=gain128[:])
+
+        for h, (weights, scale) in enumerate([(scaled_0, inv), (w_1, factor)]):
+            gated = wide("gated%d" % h)
+            nc.scalar.activation(out=gated[:], in_=weights[:], func=ACT.Tanh, scale=scale[:])
+            result = combine("result%d" % h, gated[:], base_sb[:, halves[h]], ALU.add)
+            nc.sync.dma_start(out=out[:, halves[h]], in_=result[:])

from contextlib import ExitStack

import concourse.mybir as mybir

D, T, I, Q = 512, 1024, 512, 128
FLOPS = 2 * 2 * D * T * Q

F32 = mybir.dt.float32
BF16 = mybir.dt.bfloat16
I32 = mybir.dt.int32
U32 = mybir.dt.uint32
U16 = mybir.dt.uint16
U8 = mybir.dt.uint8
FP8X4 = mybir.dt.float8_e4m3fn_x4
ALU = mybir.AluOpType
ACT = mybir.ActivationFunctionType

P = 128
PACK = 4
QUARTER = T // 4
HALF = I // 2
REACH = 2
PAD = 8
LIST_ROWS = 16


def tile_attend_exchanged_smeared_gated_heads_kernel(
    tc, query, query2, keys_words, keys_scales, lam, smear, base, gain2, offs, offs2, out
):
    nc = tc.nc
    with ExitStack() as ctx:
        pool = ctx.enter_context(tc.tile_pool(name="pool", bufs=1))
        psum = ctx.enter_context(tc.psum_pool(name="psum", bufs=1))

        def wide(name):
            return pool.tile([P, HALF], F32, name=name)

        def column(name):
            return pool.tile([P, 1], F32, name=name)

        key_scales = pool.tile([P, QUARTER], U8, name="key_scales", align_bytes=64)
        nc.vector.memset(key_scales[:].bitcast(I32), 0)

        raw = [pool.tile([P, PACK, Q], F32, name="raw%d" % s) for s in range(2)]
        words = [pool.tile([P, T // 2], I32, name="words%d" % h, align_bytes=64) for h in range(2)]
        words_hbm = keys_words[0].rearrange("p n t -> p (n t)").bitcast(I32)
        scales_hbm = keys_scales[0].bitcast(I32)
        nc.sync.dma_start(out=raw[0][:], in_=query.rearrange("(p j) q -> p j q", j=PACK))
        nc.sync.dma_start(out=words[0][:], in_=words_hbm[:, 0 : T // 2])
        for r in range(4):
            nc.sync.dma_start(
                out=key_scales[32 * r : 32 * r + 16, :].bitcast(I32),
                in_=scales_hbm[4 * r : 4 * r + 4, :].rearrange("j (c n) -> c j n", c=4),
            )
        nc.sync.dma_start(out=raw[1][:], in_=query2.rearrange("(p j) q -> p j q", j=PACK))
        nc.sync.dma_start(out=words[1][:], in_=words_hbm[:, T // 2 : T])
        first = pool.tile([P, I // LIST_ROWS], U16, name="first")
        second = pool.tile([P, I // LIST_ROWS], U16, name="second")
        nc.sync.dma_start(first[:], offs)
        nc.sync.dma_start(second[:], offs2)
        lam_sb, smear_sb, gain_sb = column("lam_sb"), column("smear_sb"), column("gain_sb")
        base_sb = pool.tile([P, I], F32, name="base_sb")
        nc.sync.dma_start(out=lam_sb[:], in_=lam)
        nc.sync.dma_start(out=smear_sb[:], in_=smear)
        nc.sync.dma_start(out=gain_sb[:], in_=gain2)
        nc.sync.dma_start(out=base_sb[:], in_=base)

        shares = [pool.tile([P, PAD + HALF + h], F32, name="shares%d" % h) for h in range(2)]
        nc.vector.memset(shares[0][:, PAD - REACH : PAD], 0.0)

        def quantise(s):
            grouped = pool.tile([P, Q, PACK], BF16, name="grouped%d" % s, align_bytes=64)
            codes = pool.tile([P, Q], U32, name="codes%d" % s, align_bytes=64)
            q_scales = pool.tile([P, Q], U8, name="q_scales%d" % s, align_bytes=64)
            runs = [slice(0, Q // 2), slice(Q // 2, Q)]
            for rows in runs:
                nc.vector.tensor_copy(
                    out=grouped[:, rows, :].rearrange("p (c i) j -> p c j i", i=4),
                    in_=raw[s][:, :, rows].rearrange("p j (c i) -> p c j i", i=4),
                )
            for rows in runs:
                nc.vector.quantize_mx(
                    out=codes[:, rows].bitcast(FP8X4),
                    scales=q_scales[:, rows],
                    in_=grouped[:, rows, :].rearrange("p q j -> p (q j)"),
                )
            return codes, q_scales

        def score(s, operand, copiers):
            codes, q_scales = operand
            table = pool.tile([P, T], F32, name="scores%d" % s)
            for c, copier in enumerate(copiers):
                h, c0 = divmod(c * QUARTER, T // 2)
                bank = psum.tile([P, QUARTER], F32, name="bank%d_%d" % (s, c))
                nc.tensor.matmul_mx(
                    out=bank[:],
                    lhsT=codes[:].bitcast(FP8X4),
                    lhsT_scale=q_scales[:],
                    rhs=words[h][:, c0 : c0 + QUARTER].bitcast(FP8X4),
                    rhs_scale=key_scales[4 * c : P, :],
                    start=True,
                    stop=True,
                )
                copier(out=table[:, c * QUARTER : (c + 1) * QUARTER], in_=bank[:])
            return table

        def listed(table, lists, i0, i1):
            return table[:].indirect(lists[:, i0 // LIST_ROWS : i1 // LIST_ROWS])

        def gather_on_vector(name, table, lists):
            got = pool.tile([P, I], F32, name=name)
            nc.vector.tensor_copy(out=got[:], in_=listed(table, lists, 0, I))
            return got

        def gather_on_scalar(name, table, lists, i0, i1):
            got = pool.tile([P, i1 - i0], F32, name=name)
            nc.scalar.activation(out=got[:], in_=listed(table, lists, i0, i1), func=ACT.Copy)
            return got

        on_scalar, on_vector = nc.scalar.copy, nc.vector.tensor_copy
        operands = [quantise(s) for s in range(2)]
        a = score(0, operands[0], [on_scalar, on_scalar, on_scalar, on_vector])
        a_first = gather_on_vector("a_first", a, first)
        b = score(1, operands[1], [on_scalar] * 4)
        a_second = gather_on_scalar("a_second", a, second, 0, I)
        b_second = gather_on_vector("b_second", b, second)
        b_first = [gather_on_scalar("b_first%d" % h, b, first, h * HALF, (h + 1) * HALF) for h in range(2)]

        neg = pool.tile([P, I + 1], F32, name="neg")
        low = [neg[:, I : I + 1], column("row_low")[:]]
        sums = [column("sum%d" % h) for h in range(2)]
        halves = [slice(h * HALF, (h + 1) * HALF) for h in range(2)]

        def combine(name, x, y, op):
            z = wide(name)
            nc.vector.tensor_tensor(out=z[:], in0=x, in1=y, op=op)
            return z

        def straight(h):
            return combine("straight%d" % h, a_first[:, halves[h]], b_second[:, halves[h]], ALU.max)

        def crossed(h):
            return combine("crossed%d" % h, a_second[:, halves[h]], b_first[h][:], ALU.max)

        def scale_and_min(h, diff):
            nc.vector.tensor_scalar(
                out=neg[:, halves[h]],
                in0=diff[:],
                scalar1=lam_sb[:],
                scalar2=low[0] if h else None,
                op0=ALU.mult,
                op1=ALU.min,
                accum_out=low[h],
            )

        def exp_of(dst, src, h, accum=None):
            nc.scalar.activation(out=dst, in_=src, func=ACT.Exp, bias=low[h], scale=-1.0, accum_out=accum)

        def smear_step(name, older, newer):
            z = wide(name)
            nc.vector.scalar_tensor_tensor(
                out=z[:], in0=older, scalar=smear_sb[:], in1=newer, op0=ALU.mult, op1=ALU.add
            )
            return z

        def shifted(h, shift):
            return shares[h][:, PAD - shift : PAD - shift + HALF]

        straight_0 = straight(0)
        straight_1 = straight(1)
        crossed_0 = crossed(0)
        diff_0 = combine("diff0", crossed_0[:], straight_0[:], ALU.subtract)
        crossed_1 = crossed(1)
        scale_and_min(0, diff_0)
        own = HALF - REACH
        exp_of(shares[0][:, PAD : PAD + own], neg[:, 0:own], 0, sums[0][:])
        exp_of(shares[0][:, PAD + own : PAD + HALF], neg[:, own:HALF], 0)
        diff_1 = combine("diff1", crossed_1[:], straight_1[:], ALU.subtract)
        scale_and_min(1, diff_1)

        back_0 = smear_step("back0", shifted(0, 2), shifted(0, 1))
        rest = column("rest")
        nc.vector.tensor_scalar(out=rest[:], in0=sums[0][:], scalar1=-1.0, scalar2=None, op0=ALU.add)
        exp_of(shares[1][:, PAD - REACH : PAD + HALF + 1], neg[:, own : I + 1], 1, sums[1][:])
        shrink = shares[1][:, PAD + HALF : PAD + HALF + 1]
        w_0 = smear_step("w0", back_0[:], shifted(0, 0))
        gain128 = column("gain128")
        nc.vector.tensor_scalar(out=gain128[:], in0=gain_sb[:], scalar1=128.0, scalar2=None, op0=ALU.mult)
        total = column("total")
        nc.scalar.activation(out=total[:], in_=rest[:], func=ACT.Identity, scale=shrink, bias=sums[1][:])
        back_1 = smear_step("back1", shifted(1, 2), shifted(1, 1))
        inv = column("inv")
        nc.vector.reciprocal(out=inv[:], in_=total[:])
        scaled_0 = wide("scaled0")
        nc.vector.tensor_scalar(
            out=scaled_0[:], in0=w_0[:], scalar1=gain128[:], scalar2=shrink, op0=ALU.mult, op1=ALU.mult
        )
        w_1 = smear_step("w1", back_1[:], shifted(1, 0))
        factor = column("factor")
        nc.scalar.activation(out=factor[:], in_=inv[:], func=ACT.Copy, scale=gain128[:])

        for h, (weights, scale) in enumerate([(scaled_0, inv), (w_1, factor)]):
            gated = wide("gated%d" % h)
            nc.scalar.activation(out=gated[:], in_=weights[:], func=ACT.Tanh, scale=scale[:])
            result = combine("result%d" % h, gated[:], base_sb[:, halves[h]], ALU.add)
            nc.sync.dma_start(out=out[:, halves[h]], in_=result[:])
